import numpy as np, ml_dtypes
CORES = [19,147,275,403]
N = 4
C = 1024
SIGN = [[1,1,1,1],[1,-1,1,-1],[1,1,-1,-1],[1,-1,-1,1]]
def setup_inputs(rng):
    return {"x": rng.standard_normal((N, 128, C), dtype=np.float32).astype(ml_dtypes.bfloat16)}
def setup_inputs_big(rng):
    d = setup_inputs(rng)
    for k in ("x",): d[k] = (d[k].astype(np.float32) * 1048576.0).astype(d[k].dtype)
    return d
def setup_inputs_small(rng):
    d = setup_inputs(rng)
    for k in ("x",): d[k] = (d[k].astype(np.float32) * (1 / 1048576.0)).astype(d[k].dtype)
    return d
def setup_inputs_apart(rng):
    d = setup_inputs(rng)
    f = (10.0 ** rng.permutation(np.linspace(-1.5, 1.5, N))).astype(np.float32).reshape(N, 1, 1)
    for k in ("x",): d[k] = (d[k].astype(np.float32) * f).astype(d[k].dtype)
    return d
def reference(x):
    X = x.astype(np.float64)
    y = np.stack([sum(SIGN[r][j] * X[j] for j in range(N)) for r in range(N)])
    return {"y": y.astype(ml_dtypes.bfloat16)}

@@ -1,0 +1,121 @@
+from concourse.bass import DstId, RemoteDMATransfer
+from concourse.mybir import AluOpType
+
+C = 1024
+W = C // 2
+
+SCRATCH = {
+    "xs": ("sbuf", [128, C], "bfloat16"),
+    "nx": ("sbuf", [128, C], "bfloat16"),
+    "r1": ("sbuf", [128, C], "bfloat16"),
+    "r2": ("sbuf", [128, C], "bfloat16"),
+    "out": ("sbuf", [128, C], "bfloat16"),
+    "zero": ("psum", [128, W], "float32"),
+    "xf": ("psum", [128, C], "float32"),
+    "own": ("psum", [128, C], "float32"),
+}
+SEMAPHORES = ["ld", "z", "ng0", "ng1", "cp", "a10", "a11", "a20", "a21", "ow0", "ow1", "fin0", "fin1", "sent", "st"]
+
+
+def _neighbours(c, cores, topo):
+    near = far = None
+    for d in cores:
+        if d == c or not topo.may_write(c, d):
+            continue
+        if topo.same_plane(c, d):
+            near = d
+        elif topo.rack(topo.host(c)) != topo.rack(topo.host(d)):
+            far = d
+    return near, far
+
+
+def _lanes(src, dst, which, topo):
+    allowed = topo.mask(src, dst)
+    bits = [b for b in range(16) if (allowed >> b) & 1]
+    return sum(1 << b for b in bits[which::2]), len(bits[which::2])
+
+
+def rank_program(g, core, T, topo):
+    r = T.rank_of(core)
+    if r is None:
+        return
+    sign = T.tables["SIGN"]
+    sem = T.sem
+    v = g.vector
+    halves = (0, 1)
+    cols = [slice(h * W, (h + 1) * W) for h in halves]
+
+    mine = _neighbours(core, T.cores, topo)
+    p = [mine[h] for h in halves]
+    q = [mine[1 - h] for h in halves]
+    rp = [T.rank_of(c) for c in p]
+    rq = [T.rank_of(c) for c in q]
+    rel = [sign[rq[h]][rp[h]] * sign[rq[h]][r] for h in halves]
+    s_m = [sign[r][T.rank_of(_neighbours(q[h], T.cores, topo)[h])] for h in halves]
+
+    def transfer(dst, link, remote_sem, srcs, out):
+        rid, pid = topo.addr(dst, core)
+        m, n = _lanes(core, dst, link, topo)
+        if len(srcs) == 1:
+            t = RemoteDMATransfer(dst_ids=[DstId(rid=rid, pnc=pid)], dma_engine_mask=m, remote_sem=remote_sem,
+                                  src=srcs[0], dst=out, alu_op=0)
+        else:
+            t = RemoteDMATransfer(dst_ids=[DstId(rid=rid, pnc=pid)], dma_engine_mask=m, remote_sem=remote_sem,
+                                  srcs=srcs, dsts=[out], alu_op=1)
+        return t, n
+
+    g.sync.dma_start(T.xs[:], T.x[:]).then_inc(sem.ld, 16)
+
+    g.wait_ge(sem.ld, 16)
+    step1 = [transfer(p[h], h, sem["a1%d" % h], [T.xs[:, cols[h]]], T.r1[:, cols[h]]) for h in halves]
+    g.remote_dma_fused([t for t, _ in step1], local_sem=sem.sent)
+    n_in1 = [_lanes(p[h], core, h, topo)[1] for h in halves]
+    n_in2 = [_lanes(q[h], core, 1 - h, topo)[1] for h in halves]
+    for h in halves:
+        g.wait_ge(sem["a1%d" % h], n_in1[h])
+        if rel[h] < 0:
+            g.wait_ge(sem["ng%d" % h], 1)
+    step2 = [transfer(q[h], 1 - h, sem["a2%d" % h],
+                      [T.r1[:, cols[h]], (T.xs if rel[h] > 0 else T.nx)[:, cols[h]]], T.r2[:, cols[h]]) for h in halves]
+    g.remote_dma_fused([t for t, _ in step2], local_sem=sem.sent)
+
+    if min(rel) < 0:
+        v.memset(T.zero[:], 0.0).then_inc(sem.z, 1)
+        v.wait_ge(sem.z, 1)
+    v.wait_ge(sem.ld, 16)
+    for h in halves:
+        if rel[h] < 0:
+            v.tensor_tensor(T.nx[:, cols[h]], T.zero[:], T.xs[:, cols[h]], AluOpType.subtract).then_inc(sem["ng%d" % h], 1)
+    for h in halves:
+        v.tensor_copy(T.xf[:, cols[h]], T.xs[:, cols[h]]).then_inc(sem.cp, 1)
+    v.wait_ge(sem.cp, 2)
+    s_o = [1, 1]
+    for h in halves:
+        a, b = sign[r][r], sign[r][rp[h]]
+        mine_f, got = T.xf[:, cols[h]], T.r1[:, cols[h]]
+        v.wait_ge(sem["a1%d" % h], n_in1[h])
+        if a > 0:
+            i = v.tensor_tensor(T.own[:, cols[h]], mine_f, got, AluOpType.add if b > 0 else AluOpType.subtract)
+        elif b > 0:
+            i = v.tensor_tensor(T.own[:, cols[h]], got, mine_f, AluOpType.subtract)
+        else:
+            i = v.tensor_tensor(T.own[:, cols[h]], mine_f, got, AluOpType.add)
+            s_o[h] = -1
+        i.then_inc(sem["ow%d" % h], 1)
+    for h in halves:
+        assert s_o[h] > 0 or s_m[h] > 0
+        part, got = T.own[:, cols[h]], T.r2[:, cols[h]]
+        v.wait_ge(sem["ow%d" % h], 1)
+        v.wait_ge(sem["a2%d" % h], n_in2[h])
+        if s_o[h] > 0:
+            i = v.tensor_tensor(T.out[:, cols[h]], part, got, AluOpType.add if s_m[h] > 0 else AluOpType.subtract)
+        else:
+            i = v.tensor_tensor(T.out[:, cols[h]], got, part, AluOpType.subtract)
+        i.then_inc(sem["fin%d" % h], 1)
+
+    for h, queue in zip(halves, (g.sync, g.scalar)):
+        queue.wait_ge(sem["fin%d" % h], 1)
+        queue.dma_start(T.y[:, cols[h]], T.out[:, cols[h]]).then_inc(sem.st, 16)
+
+    g.wait_ge(sem.sent, sum(n for _, n in step1) + sum(n for _, n in step2))
+    g.wait_ge(sem.st, 32)

@@ -2,7 +2,9 @@ from concourse.bass import DstId, RemoteDMATransfer
 from concourse.mybir import AluOpType
 
 C = 1024
-W = C // 2
+NCH = 2
+WC = C // NCH
+WP = WC // 2
 
 SCRATCH = {
     "xs": ("sbuf", [128, C], "bfloat16"),
@@ -10,11 +12,11 @@ SCRATCH = {
     "r1": ("sbuf", [128, C], "bfloat16"),
     "r2": ("sbuf", [128, C], "bfloat16"),
     "out": ("sbuf", [128, C], "bfloat16"),
-    "zero": ("psum", [128, W], "float32"),
+    "zero": ("psum", [128, WP], "float32"),
     "xf": ("psum", [128, C], "float32"),
     "own": ("psum", [128, C], "float32"),
 }
-SEMAPHORES = ["ld", "z", "ng0", "ng1", "cp", "a10", "a11", "a20", "a21", "ow0", "ow1", "fin0", "fin1", "sent", "st"]
+SEMAPHORES = ["z", "sent", "st"] + [n + str(c) for c in range(NCH) for n in ("ld", "ng", "cp", "a1_", "a2_", "ow", "fin")]
 
 
 def _neighbours(c, cores, topo):
@@ -42,80 +44,90 @@ def rank_program(g, core, T, topo):
     sign = T.tables["SIGN"]
     sem = T.sem
     v = g.vector
-    halves = (0, 1)
-    cols = [slice(h * W, (h + 1) * W) for h in halves]
+    pieces = (0, 1)
+    chunks = range(NCH)
+    queues = (g.sync, g.scalar)
+    ccols = [slice(c * WC, (c + 1) * WC) for c in chunks]
+    cols = [[slice(c * WC + h * WP, c * WC + (h + 1) * WP) for h in pieces] for c in chunks]
 
     mine = _neighbours(core, T.cores, topo)
-    p = [mine[h] for h in halves]
-    q = [mine[1 - h] for h in halves]
+    p = [mine[h] for h in pieces]
+    q = [mine[1 - h] for h in pieces]
     rp = [T.rank_of(c) for c in p]
     rq = [T.rank_of(c) for c in q]
-    rel = [sign[rq[h]][rp[h]] * sign[rq[h]][r] for h in halves]
-    s_m = [sign[r][T.rank_of(_neighbours(q[h], T.cores, topo)[h])] for h in halves]
+    rel = [sign[rq[h]][rp[h]] * sign[rq[h]][r] for h in pieces]
+    n_neg = sum(1 for h in pieces if rel[h] < 0)
+    s_m = [sign[r][T.rank_of(_neighbours(q[h], T.cores, topo)[h])] for h in pieces]
+    n_in1 = sum(_lanes(p[h], core, h, topo)[1] for h in pieces)
+    n_in2 = sum(_lanes(q[h], core, 1 - h, topo)[1] for h in pieces)
+    n_out = [0]
 
     def transfer(dst, link, remote_sem, srcs, out):
         rid, pid = topo.addr(dst, core)
         m, n = _lanes(core, dst, link, topo)
+        n_out[0] += n
         if len(srcs) == 1:
-            t = RemoteDMATransfer(dst_ids=[DstId(rid=rid, pnc=pid)], dma_engine_mask=m, remote_sem=remote_sem,
-                                  src=srcs[0], dst=out, alu_op=0)
-        else:
-            t = RemoteDMATransfer(dst_ids=[DstId(rid=rid, pnc=pid)], dma_engine_mask=m, remote_sem=remote_sem,
-                                  srcs=srcs, dsts=[out], alu_op=1)
-        return t, n
+            return RemoteDMATransfer(dst_ids=[DstId(rid=rid, pnc=pid)], dma_engine_mask=m, remote_sem=remote_sem,
+                                     src=srcs[0], dst=out, alu_op=0)
+        return RemoteDMATransfer(dst_ids=[DstId(rid=rid, pnc=pid)], dma_engine_mask=m, remote_sem=remote_sem,
+                                 srcs=srcs, dsts=[out], alu_op=1)
 
-    g.sync.dma_start(T.xs[:], T.x[:]).then_inc(sem.ld, 16)
+    for c in chunks:
+        queues[c % 2].dma_start(T.xs[:, ccols[c]], T.x[:, ccols[c]]).then_inc(sem["ld%d" % c], 16)
 
-    g.wait_ge(sem.ld, 16)
-    step1 = [transfer(p[h], h, sem["a1%d" % h], [T.xs[:, cols[h]]], T.r1[:, cols[h]]) for h in halves]
-    g.remote_dma_fused([t for t, _ in step1], local_sem=sem.sent)
-    n_in1 = [_lanes(p[h], core, h, topo)[1] for h in halves]
-    n_in2 = [_lanes(q[h], core, 1 - h, topo)[1] for h in halves]
-    for h in halves:
-        g.wait_ge(sem["a1%d" % h], n_in1[h])
-        if rel[h] < 0:
-            g.wait_ge(sem["ng%d" % h], 1)
-    step2 = [transfer(q[h], 1 - h, sem["a2%d" % h],
-                      [T.r1[:, cols[h]], (T.xs if rel[h] > 0 else T.nx)[:, cols[h]]], T.r2[:, cols[h]]) for h in halves]
-    g.remote_dma_fused([t for t, _ in step2], local_sem=sem.sent)
+    for c in chunks:
+        g.wait_ge(sem["ld%d" % c], 16)
+        g.remote_dma_fused([transfer(p[h], h, sem["a1_%d" % c], [T.xs[:, cols[c][h]]], T.r1[:, cols[c][h]])
+                            for h in pieces], local_sem=sem.sent)
+    for c in chunks:
+        g.wait_ge(sem["a1_%d" % c], n_in1)
+        if n_neg:
+            g.wait_ge(sem["ng%d" % c], n_neg)
+        g.remote_dma_fused([transfer(q[h], 1 - h, sem["a2_%d" % c],
+                                     [T.r1[:, cols[c][h]], (T.xs if rel[h] > 0 else T.nx)[:, cols[c][h]]],
+                                     T.r2[:, cols[c][h]]) for h in pieces], local_sem=sem.sent)
 
-    if min(rel) < 0:
+    if n_neg:
         v.memset(T.zero[:], 0.0).then_inc(sem.z, 1)
         v.wait_ge(sem.z, 1)
-    v.wait_ge(sem.ld, 16)
-    for h in halves:
-        if rel[h] < 0:
-            v.tensor_tensor(T.nx[:, cols[h]], T.zero[:], T.xs[:, cols[h]], AluOpType.subtract).then_inc(sem["ng%d" % h], 1)
-    for h in halves:
-        v.tensor_copy(T.xf[:, cols[h]], T.xs[:, cols[h]]).then_inc(sem.cp, 1)
-    v.wait_ge(sem.cp, 2)
+    for c in chunks:
+        v.wait_ge(sem["ld%d" % c], 16)
+        for h in pieces:
+            if rel[h] < 0:
+                v.tensor_tensor(T.nx[:, cols[c][h]], T.zero[:], T.xs[:, cols[c][h]],
+                                AluOpType.subtract).then_inc(sem["ng%d" % c], 1)
+    for c in chunks:
+        v.tensor_copy(T.xf[:, ccols[c]], T.xs[:, ccols[c]]).then_inc(sem["cp%d" % c], 1)
     s_o = [1, 1]
-    for h in halves:
-        a, b = sign[r][r], sign[r][rp[h]]
-        mine_f, got = T.xf[:, cols[h]], T.r1[:, cols[h]]
-        v.wait_ge(sem["a1%d" % h], n_in1[h])
-        if a > 0:
-            i = v.tensor_tensor(T.own[:, cols[h]], mine_f, got, AluOpType.add if b > 0 else AluOpType.subtract)
-        elif b > 0:
-            i = v.tensor_tensor(T.own[:, cols[h]], got, mine_f, AluOpType.subtract)
-        else:
-            i = v.tensor_tensor(T.own[:, cols[h]], mine_f, got, AluOpType.add)
-            s_o[h] = -1
-        i.then_inc(sem["ow%d" % h], 1)
-    for h in halves:
-        assert s_o[h] > 0 or s_m[h] > 0
-        part, got = T.own[:, cols[h]], T.r2[:, cols[h]]
-        v.wait_ge(sem["ow%d" % h], 1)
-        v.wait_ge(sem["a2%d" % h], n_in2[h])
-        if s_o[h] > 0:
-            i = v.tensor_tensor(T.out[:, cols[h]], part, got, AluOpType.add if s_m[h] > 0 else AluOpType.subtract)
-        else:
-            i = v.tensor_tensor(T.out[:, cols[h]], got, part, AluOpType.subtract)
-        i.then_inc(sem["fin%d" % h], 1)
+    for c in chunks:
+        v.wait_ge(sem["cp%d" % c], 1)
+        v.wait_ge(sem["a1_%d" % c], n_in1)
+        for h in pieces:
+            a, b = sign[r][r], sign[r][rp[h]]
+            mine_f, got, res = T.xf[:, cols[c][h]], T.r1[:, cols[c][h]], T.own[:, cols[c][h]]
+            if a > 0:
+                i = v.tensor_tensor(res, mine_f, got, AluOpType.add if b > 0 else AluOpType.subtract)
+            elif b > 0:
+                i = v.tensor_tensor(res, got, mine_f, AluOpType.subtract)
+            else:
+                i = v.tensor_tensor(res, mine_f, got, AluOpType.add)
+                s_o[h] = -1
+            i.then_inc(sem["ow%d" % c], 1)
+    for c in chunks:
+        v.wait_ge(sem["ow%d" % c], 2)
+        v.wait_ge(sem["a2_%d" % c], n_in2)
+        for h in pieces:
+            assert s_o[h] > 0 or s_m[h] > 0
+            part, got, res = T.own[:, cols[c][h]], T.r2[:, cols[c][h]], T.out[:, cols[c][h]]
+            if s_o[h] > 0:
+                i = v.tensor_tensor(res, part, got, AluOpType.add if s_m[h] > 0 else AluOpType.subtract)
+            else:
+                i = v.tensor_tensor(res, got, part, AluOpType.subtract)
+            i.then_inc(sem["fin%d" % c], 1)
 
-    for h, queue in zip(halves, (g.sync, g.scalar)):
-        queue.wait_ge(sem["fin%d" % h], 1)
-        queue.dma_start(T.y[:, cols[h]], T.out[:, cols[h]]).then_inc(sem.st, 16)
+    for c in chunks:
+        queues[c % 2].wait_ge(sem["fin%d" % c], 2)
+        queues[c % 2].dma_start(T.y[:, ccols[c]], T.out[:, ccols[c]]).then_inc(sem.st, 16)
 
-    g.wait_ge(sem.sent, sum(n for _, n in step1) + sum(n for _, n in step2))
-    g.wait_ge(sem.st, 32)
+    g.wait_ge(sem.sent, n_out[0])
+    g.wait_ge(sem.st, 16 * NCH)

@@ -2,9 +2,11 @@ from concourse.bass import DstId, RemoteDMATransfer
 from concourse.mybir import AluOpType
 
 C = 1024
-NCH = 2
-WC = C // NCH
-WP = WC // 2
+WORLD = 512
+PARTS = ((0, 512), (512, 768), (768, 1024))
+NP = len(PARTS)
+B = NP - 1
+WZ = max((b - a) // 2 for a, b in PARTS)
 
 SCRATCH = {
     "xs": ("sbuf", [128, C], "bfloat16"),
@@ -12,11 +14,12 @@ SCRATCH = {
     "r1": ("sbuf", [128, C], "bfloat16"),
     "r2": ("sbuf", [128, C], "bfloat16"),
     "out": ("sbuf", [128, C], "bfloat16"),
-    "zero": ("psum", [128, WP], "float32"),
+    "zero": ("psum", [128, WZ], "float32"),
     "xf": ("psum", [128, C], "float32"),
     "own": ("psum", [128, C], "float32"),
 }
-SEMAPHORES = ["z", "sent", "st"] + [n + str(c) for c in range(NCH) for n in ("ld", "ng", "cp", "a1_", "a2_", "ow", "fin")]
+SEMAPHORES = ["z", "sent", "st", "hx", "h1"] + [n + str(c) for c in range(NP)
+                                                for n in ("ld", "ng", "cp", "a1_", "a2_", "ow", "fin")]
 
 
 def _neighbours(c, cores, topo):
@@ -31,26 +34,43 @@ def _neighbours(c, cores, topo):
     return near, far
 
 
+def _helper(c, topo):
+    for k in range(WORLD):
+        if topo.host(k) == topo.host(c) and topo.chip(k) == topo.chip(c) and topo.die(k) != topo.die(c):
+            return k
+    return None
+
+
 def _lanes(src, dst, which, topo):
     allowed = topo.mask(src, dst)
     bits = [b for b in range(16) if (allowed >> b) & 1]
-    return sum(1 << b for b in bits[which::2]), len(bits[which::2])
+    sel = bits[which::2]
+    return sum(1 << b for b in sel), len(sel)
+
+
+def _chip_lanes(src, dst, off, topo):
+    allowed = topo.mask(src, dst) & ~topo.mask(src, off)
+    bits = [b for b in range(16) if (allowed >> b) & 1]
+    sel = bits[0::2]
+    return sum(1 << b for b in sel), len(sel)
 
 
 def rank_program(g, core, T, topo):
-    r = T.rank_of(core)
-    if r is None:
+    helper_of = {c: _helper(c, topo) for c in T.cores}
+    owner = {h: c for c, h in helper_of.items()}
+    if T.rank_of(core) is None and core not in owner:
         return
+    me = core if T.rank_of(core) is not None else owner[core]
+    r = T.rank_of(me)
     sign = T.tables["SIGN"]
     sem = T.sem
     v = g.vector
     pieces = (0, 1)
-    chunks = range(NCH)
-    queues = (g.sync, g.scalar)
-    ccols = [slice(c * WC, (c + 1) * WC) for c in chunks]
-    cols = [[slice(c * WC + h * WP, c * WC + (h + 1) * WP) for h in pieces] for c in chunks]
+    pcols = [slice(a, b) for a, b in PARTS]
+    cols = [[slice(a + h * (b - a) // 2, a + (h + 1) * (b - a) // 2) for h in pieces] for a, b in PARTS]
+    wid = [(b - a) // 2 for a, b in PARTS]
 
-    mine = _neighbours(core, T.cores, topo)
+    mine = _neighbours(me, T.cores, topo)
     p = [mine[h] for h in pieces]
     q = [mine[1 - h] for h in pieces]
     rp = [T.rank_of(c) for c in p]
@@ -58,13 +78,11 @@ def rank_program(g, core, T, topo):
     rel = [sign[rq[h]][rp[h]] * sign[rq[h]][r] for h in pieces]
     n_neg = sum(1 for h in pieces if rel[h] < 0)
     s_m = [sign[r][T.rank_of(_neighbours(q[h], T.cores, topo)[h])] for h in pieces]
-    n_in1 = sum(_lanes(p[h], core, h, topo)[1] for h in pieces)
-    n_in2 = sum(_lanes(q[h], core, 1 - h, topo)[1] for h in pieces)
     n_out = [0]
 
-    def transfer(dst, link, remote_sem, srcs, out):
+    def transfer(dst, lanes, remote_sem, srcs, out):
         rid, pid = topo.addr(dst, core)
-        m, n = _lanes(core, dst, link, topo)
+        m, n = lanes
         n_out[0] += n
         if len(srcs) == 1:
             return RemoteDMATransfer(dst_ids=[DstId(rid=rid, pnc=pid)], dma_engine_mask=m, remote_sem=remote_sem,
@@ -72,36 +90,71 @@ def rank_program(g, core, T, topo):
         return RemoteDMATransfer(dst_ids=[DstId(rid=rid, pnc=pid)], dma_engine_mask=m, remote_sem=remote_sem,
                                  srcs=srcs, dsts=[out], alu_op=1)
 
-    for c in chunks:
-        queues[c % 2].dma_start(T.xs[:, ccols[c]], T.x[:, ccols[c]]).then_inc(sem["ld%d" % c], 16)
+    def negate(c, ready, count):
+        v.wait_ge(ready, count)
+        for h in pieces:
+            if rel[h] < 0:
+                v.tensor_tensor(T.nx[:, cols[c][h]], T.zero[:, 0:wid[c]], T.xs[:, cols[c][h]],
+                                AluOpType.subtract).then_inc(sem["ng%d" % c], 1)
 
-    for c in chunks:
-        g.wait_ge(sem["ld%d" % c], 16)
-        g.remote_dma_fused([transfer(p[h], h, sem["a1_%d" % c], [T.xs[:, cols[c][h]]], T.r1[:, cols[c][h]])
-                            for h in pieces], local_sem=sem.sent)
-    for c in chunks:
-        g.wait_ge(sem["a1_%d" % c], n_in1)
-        if n_neg:
-            g.wait_ge(sem["ng%d" % c], n_neg)
-        g.remote_dma_fused([transfer(q[h], 1 - h, sem["a2_%d" % c],
-                                     [T.r1[:, cols[c][h]], (T.xs if rel[h] > 0 else T.nx)[:, cols[c][h]]],
-                                     T.r2[:, cols[c][h]]) for h in pieces], local_sem=sem.sent)
+    def fold_srcs(c, h):
+        return [T.r1[:, cols[c][h]], (T.xs if rel[h] > 0 else T.nx)[:, cols[c][h]]]
 
     if n_neg:
         v.memset(T.zero[:], 0.0).then_inc(sem.z, 1)
         v.wait_ge(sem.z, 1)
-    for c in chunks:
-        v.wait_ge(sem["ld%d" % c], 16)
-        for h in pieces:
-            if rel[h] < 0:
-                v.tensor_tensor(T.nx[:, cols[c][h]], T.zero[:], T.xs[:, cols[c][h]],
-                                AluOpType.subtract).then_inc(sem["ng%d" % c], 1)
-    for c in chunks:
-        v.tensor_copy(T.xf[:, ccols[c]], T.xs[:, ccols[c]]).then_inc(sem["cp%d" % c], 1)
+
+    if core != me:
+        n_hx = _chip_lanes(me, core, p[0], topo)[1]
+        n_h1 = sum(_lanes(helper_of[p[h]], core, h, topo)[1] for h in pieces)
+        g.wait_ge(sem.hx, n_hx)
+        g.remote_dma_fused([transfer(helper_of[p[h]], _lanes(core, helper_of[p[h]], h, topo), sem.h1,
+                                     [T.xs[:, cols[B][h]]], T.r1[:, cols[B][h]]) for h in pieces], local_sem=sem.sent)
+        negate(B, sem.hx, n_hx)
+        g.wait_ge(sem.h1, n_h1)
+        if n_neg:
+            g.wait_ge(sem["ng%d" % B], n_neg)
+        g.remote_dma_fused([transfer(q[h], _lanes(core, q[h], 1 - h, topo), sem["a2_%d" % B],
+                                     fold_srcs(B, h), T.r2[:, cols[B][h]]) for h in pieces], local_sem=sem.sent)
+        g.remote_dma_fused([transfer(me, _chip_lanes(core, me, q[0], topo), sem["a1_%d" % B],
+                                     [T.r1[:, pcols[B]]], T.r1[:, pcols[B]])], local_sem=sem.sent)
+        g.wait_ge(sem.sent, n_out[0])
+        return
+
+    hlp = helper_of[core]
+    own_parts = [c for c in range(NP) if c != B]
+    n_in1 = [sum(_lanes(p[h], core, h, topo)[1] for h in pieces)] * NP
+    n_in1[B] = _chip_lanes(hlp, core, q[0], topo)[1]
+    n_in2 = [sum(_lanes(q[h], core, 1 - h, topo)[1] for h in pieces)] * NP
+    n_in2[B] = sum(_lanes(helper_of[q[h]], core, 1 - h, topo)[1] for h in pieces)
+
+    g.sync.dma_start(T.xs[:, pcols[B]], T.x[:, pcols[B]]).then_inc(sem["ld%d" % B], 16)
+    g.scalar.dma_start(T.xs[:, pcols[0]], T.x[:, pcols[0]]).then_inc(sem["ld0"], 16)
+    g.sync.dma_start(T.xs[:, pcols[1]], T.x[:, pcols[1]]).then_inc(sem["ld1"], 16)
+
+    g.wait_ge(sem["ld%d" % B], 16)
+    g.remote_dma_fused([transfer(hlp, _chip_lanes(core, hlp, p[0], topo), sem.hx,
+                                 [T.xs[:, pcols[B]]], T.xs[:, pcols[B]])], local_sem=sem.sent)
+    for c in own_parts:
+        g.wait_ge(sem["ld%d" % c], 16)
+        g.remote_dma_fused([transfer(p[h], _lanes(core, p[h], h, topo), sem["a1_%d" % c],
+                                     [T.xs[:, cols[c][h]]], T.r1[:, cols[c][h]]) for h in pieces], local_sem=sem.sent)
+    for c in own_parts:
+        g.wait_ge(sem["a1_%d" % c], n_in1[c])
+        if n_neg:
+            g.wait_ge(sem["ng%d" % c], n_neg)
+        g.remote_dma_fused([transfer(q[h], _lanes(core, q[h], 1 - h, topo), sem["a2_%d" % c],
+                                     fold_srcs(c, h), T.r2[:, cols[c][h]]) for h in pieces], local_sem=sem.sent)
+
+    for c in own_parts:
+        negate(c, sem["ld%d" % c], 16)
+    v.wait_ge(sem["ld%d" % B], 16)
+    for c in range(NP):
+        v.tensor_copy(T.xf[:, pcols[c]], T.xs[:, pcols[c]]).then_inc(sem["cp%d" % c], 1)
     s_o = [1, 1]
-    for c in chunks:
+    for c in range(NP):
         v.wait_ge(sem["cp%d" % c], 1)
-        v.wait_ge(sem["a1_%d" % c], n_in1)
+        v.wait_ge(sem["a1_%d" % c], n_in1[c])
         for h in pieces:
             a, b = sign[r][r], sign[r][rp[h]]
             mine_f, got, res = T.xf[:, cols[c][h]], T.r1[:, cols[c][h]], T.own[:, cols[c][h]]
@@ -113,9 +166,9 @@ def rank_program(g, core, T, topo):
                 i = v.tensor_tensor(res, mine_f, got, AluOpType.add)
                 s_o[h] = -1
             i.then_inc(sem["ow%d" % c], 1)
-    for c in chunks:
+    for c in (0, B, 1):
         v.wait_ge(sem["ow%d" % c], 2)
-        v.wait_ge(sem["a2_%d" % c], n_in2)
+        v.wait_ge(sem["a2_%d" % c], n_in2[c])
         for h in pieces:
             assert s_o[h] > 0 or s_m[h] > 0
             part, got, res = T.own[:, cols[c][h]], T.r2[:, cols[c][h]], T.out[:, cols[c][h]]
@@ -125,9 +178,9 @@ def rank_program(g, core, T, topo):
                 i = v.tensor_tensor(res, got, part, AluOpType.subtract)
             i.then_inc(sem["fin%d" % c], 1)
 
-    for c in chunks:
-        queues[c % 2].wait_ge(sem["fin%d" % c], 2)
-        queues[c % 2].dma_start(T.y[:, ccols[c]], T.out[:, ccols[c]]).then_inc(sem.st, 16)
+    for c, qu in ((0, g.sync), (B, g.scalar), (1, g.sync)):
+        qu.wait_ge(sem["fin%d" % c], 2)
+        qu.dma_start(T.y[:, pcols[c]], T.out[:, pcols[c]]).then_inc(sem.st, 16)
 
     g.wait_ge(sem.sent, n_out[0])
-    g.wait_ge(sem.st, 16 * NCH)
+    g.wait_ge(sem.st, 16 * NP)

@@ -3,9 +3,10 @@ from concourse.mybir import AluOpType
 
 C = 1024
 WORLD = 512
-PARTS = ((0, 512), (512, 768), (768, 1024))
+PARTS = ((384, 640), (0, 192), (192, 384), (640, 832), (832, 1024))
+NA = 2
 NP = len(PARTS)
-B = NP - 1
+NH = NP - NA
 WZ = max((b - a) // 2 for a, b in PARTS)
 
 SCRATCH = {
@@ -18,8 +19,8 @@ SCRATCH = {
     "xf": ("psum", [128, C], "float32"),
     "own": ("psum", [128, C], "float32"),
 }
-SEMAPHORES = ["z", "sent", "st", "hx", "h1"] + [n + str(c) for c in range(NP)
-                                                for n in ("ld", "ng", "cp", "a1_", "a2_", "ow", "fin")]
+SEMAPHORES = ["z", "sent", "st", "hx", "h1", "ldb"] + [n + str(c) for c in range(NP)
+                                                       for n in ("ld", "ng", "cp", "a1_", "a2_", "ow", "fin")]
 
 
 def _neighbours(c, cores, topo):
@@ -34,33 +35,51 @@ def _neighbours(c, cores, topo):
     return near, far
 
 
-def _helper(c, topo):
-    for k in range(WORLD):
-        if topo.host(k) == topo.host(c) and topo.chip(k) == topo.chip(c) and topo.die(k) != topo.die(c):
-            return k
-    return None
+def _helpers(c, topo):
+    chip = [k for k in range(WORLD) if topo.host(k) == topo.host(c) and topo.chip(k) == topo.chip(c)]
+    mate = [k for k in range(WORLD) if topo.mates(c, k)][0]
+
+    def kind(k):
+        return (topo.die(k) != topo.die(c), not topo.may_write(k, mate))
+
+    first = {}
+    for k in chip:
+        if kind(k) != kind(c) and kind(k) not in first:
+            first[kind(k)] = k
+    return [first[kd] for kd in sorted(first)]
+
+
+def _bits(m):
+    return [b for b in range(16) if (m >> b) & 1]
+
+
+def _pack(sel):
+    return sum(1 << b for b in sel), len(sel)
 
 
 def _lanes(src, dst, which, topo):
-    allowed = topo.mask(src, dst)
-    bits = [b for b in range(16) if (allowed >> b) & 1]
-    sel = bits[which::2]
-    return sum(1 << b for b in sel), len(sel)
+    return _pack(_bits(topo.mask(src, dst))[which::2])
 
 
-def _chip_lanes(src, dst, off, topo):
-    allowed = topo.mask(src, dst) & ~topo.mask(src, off)
-    bits = [b for b in range(16) if (allowed >> b) & 1]
-    sel = bits[0::2]
-    return sum(1 << b for b in sel), len(sel)
+def _hand_lanes(c, helpers, j, off, topo):
+    h = helpers[j]
+    outer = topo.mask(c, off)
+    if topo.die(h) == topo.die(c):
+        return _pack(_bits(topo.mask(c, h) & outer))
+    others = [k for k in helpers if topo.die(k) != topo.die(c)]
+    return _pack(_bits(topo.mask(c, h) & ~outer)[others.index(h)::len(others)])
+
+
+def _back_lanes(h, c, off, topo):
+    return _pack(_bits(topo.mask(h, c) & ~topo.mask(h, off)))
 
 
 def rank_program(g, core, T, topo):
-    helper_of = {c: _helper(c, topo) for c in T.cores}
-    owner = {h: c for c, h in helper_of.items()}
+    helpers_of = {c: _helpers(c, topo) for c in T.cores}
+    owner = {h: (c, j) for c, hs in helpers_of.items() for j, h in enumerate(hs)}
     if T.rank_of(core) is None and core not in owner:
         return
-    me = core if T.rank_of(core) is not None else owner[core]
+    me = core if T.rank_of(core) is not None else owner[core][0]
     r = T.rank_of(me)
     sign = T.tables["SIGN"]
     sem = T.sem
@@ -105,55 +124,57 @@ def rank_program(g, core, T, topo):
         v.wait_ge(sem.z, 1)
 
     if core != me:
-        n_hx = _chip_lanes(me, core, p[0], topo)[1]
-        n_h1 = sum(_lanes(helper_of[p[h]], core, h, topo)[1] for h in pieces)
+        j = owner[core][1]
+        c = NA + j
+        peer = [helpers_of[p[h]][j] for h in pieces]
+        n_hx = _hand_lanes(me, helpers_of[me], j, p[0], topo)[1]
+        n_h1 = sum(_lanes(peer[h], core, h, topo)[1] for h in pieces)
         g.wait_ge(sem.hx, n_hx)
-        g.remote_dma_fused([transfer(helper_of[p[h]], _lanes(core, helper_of[p[h]], h, topo), sem.h1,
-                                     [T.xs[:, cols[B][h]]], T.r1[:, cols[B][h]]) for h in pieces], local_sem=sem.sent)
-        negate(B, sem.hx, n_hx)
+        g.remote_dma_fused([transfer(peer[h], _lanes(core, peer[h], h, topo), sem.h1,
+                                     [T.xs[:, cols[c][h]]], T.r1[:, cols[c][h]]) for h in pieces], local_sem=sem.sent)
+        negate(c, sem.hx, n_hx)
         g.wait_ge(sem.h1, n_h1)
         if n_neg:
-            g.wait_ge(sem["ng%d" % B], n_neg)
-        g.remote_dma_fused([transfer(q[h], _lanes(core, q[h], 1 - h, topo), sem["a2_%d" % B],
-                                     fold_srcs(B, h), T.r2[:, cols[B][h]]) for h in pieces], local_sem=sem.sent)
-        g.remote_dma_fused([transfer(me, _chip_lanes(core, me, q[0], topo), sem["a1_%d" % B],
-                                     [T.r1[:, pcols[B]]], T.r1[:, pcols[B]])], local_sem=sem.sent)
+            g.wait_ge(sem["ng%d" % c], n_neg)
+        g.remote_dma_fused([transfer(q[h], _lanes(core, q[h], 1 - h, topo), sem["a2_%d" % c],
+                                     fold_srcs(c, h), T.r2[:, cols[c][h]]) for h in pieces], local_sem=sem.sent)
+        g.remote_dma_fused([transfer(me, _back_lanes(core, me, q[0], topo), sem["a1_%d" % c],
+                                     [T.r1[:, pcols[c]]], T.r1[:, pcols[c]])], local_sem=sem.sent)
         g.wait_ge(sem.sent, n_out[0])
         return
 
-    hlp = helper_of[core]
-    own_parts = [c for c in range(NP) if c != B]
-    n_in1 = [sum(_lanes(p[h], core, h, topo)[1] for h in pieces)] * NP
-    n_in1[B] = _chip_lanes(hlp, core, q[0], topo)[1]
-    n_in2 = [sum(_lanes(q[h], core, 1 - h, topo)[1] for h in pieces)] * NP
-    n_in2[B] = sum(_lanes(helper_of[q[h]], core, 1 - h, topo)[1] for h in pieces)
+    hs = helpers_of[core]
+    n_in1 = [sum(_lanes(p[h], core, h, topo)[1] for h in pieces)] * NA
+    n_in2 = [sum(_lanes(q[h], core, 1 - h, topo)[1] for h in pieces)] * NA
+    for j in range(NH):
+        n_in1.append(_back_lanes(hs[j], core, q[0], topo)[1])
+        n_in2.append(sum(_lanes(helpers_of[q[h]][j], core, 1 - h, topo)[1] for h in pieces))
 
-    g.sync.dma_start(T.xs[:, pcols[B]], T.x[:, pcols[B]]).then_inc(sem["ld%d" % B], 16)
-    g.scalar.dma_start(T.xs[:, pcols[0]], T.x[:, pcols[0]]).then_inc(sem["ld0"], 16)
-    g.sync.dma_start(T.xs[:, pcols[1]], T.x[:, pcols[1]]).then_inc(sem["ld1"], 16)
+    b12 = slice(PARTS[NA + 1][0], PARTS[NA + 2][1])
+    g.sync.dma_start(T.xs[:, b12], T.x[:, b12]).then_inc(sem.ldb, 16)
+    g.scalar.dma_start(T.xs[:, pcols[NA]], T.x[:, pcols[NA]]).then_inc(sem.ldb, 16)
+    g.scalar.dma_start(T.xs[:, pcols[0]], T.x[:, pcols[0]]).then_inc(sem.ld0, 16)
+    g.sync.dma_start(T.xs[:, pcols[1]], T.x[:, pcols[1]]).then_inc(sem.ld1, 16)
 
-    g.wait_ge(sem["ld%d" % B], 16)
-    g.remote_dma_fused([transfer(hlp, _chip_lanes(core, hlp, p[0], topo), sem.hx,
-                                 [T.xs[:, pcols[B]]], T.xs[:, pcols[B]])], local_sem=sem.sent)
-    for c in own_parts:
+    g.wait_ge(sem.ldb, 32)
+    g.remote_dma_fused([transfer(hs[j], _hand_lanes(core, hs, j, p[0], topo), sem.hx,
+                                 [T.xs[:, pcols[NA + j]]], T.xs[:, pcols[NA + j]]) for j in range(NH)],
+                       local_sem=sem.sent)
+    for c in range(NA):
         g.wait_ge(sem["ld%d" % c], 16)
         g.remote_dma_fused([transfer(p[h], _lanes(core, p[h], h, topo), sem["a1_%d" % c],
                                      [T.xs[:, cols[c][h]]], T.r1[:, cols[c][h]]) for h in pieces], local_sem=sem.sent)
-    for c in own_parts:
+    for c in range(NA):
         g.wait_ge(sem["a1_%d" % c], n_in1[c])
         if n_neg:
             g.wait_ge(sem["ng%d" % c], n_neg)
         g.remote_dma_fused([transfer(q[h], _lanes(core, q[h], 1 - h, topo), sem["a2_%d" % c],
                                      fold_srcs(c, h), T.r2[:, cols[c][h]]) for h in pieces], local_sem=sem.sent)
 
-    for c in own_parts:
-        negate(c, sem["ld%d" % c], 16)
-    v.wait_ge(sem["ld%d" % B], 16)
-    for c in range(NP):
-        v.tensor_copy(T.xf[:, pcols[c]], T.xs[:, pcols[c]]).then_inc(sem["cp%d" % c], 1)
     s_o = [1, 1]
-    for c in range(NP):
-        v.wait_ge(sem["cp%d" % c], 1)
+
+    def own(c):
+        v.wait_ge(sem["cp%d" % c], 2)
         v.wait_ge(sem["a1_%d" % c], n_in1[c])
         for h in pieces:
             a, b = sign[r][r], sign[r][rp[h]]
@@ -166,7 +187,8 @@ def rank_program(g, core, T, topo):
                 i = v.tensor_tensor(res, mine_f, got, AluOpType.add)
                 s_o[h] = -1
             i.then_inc(sem["ow%d" % c], 1)
-    for c in (0, B, 1):
+
+    def last(c):
         v.wait_ge(sem["ow%d" % c], 2)
         v.wait_ge(sem["a2_%d" % c], n_in2[c])
         for h in pieces:
@@ -178,7 +200,22 @@ def rank_program(g, core, T, topo):
                 i = v.tensor_tensor(res, got, part, AluOpType.subtract)
             i.then_inc(sem["fin%d" % c], 1)
 
-    for c, qu in ((0, g.sync), (B, g.scalar), (1, g.sync)):
+    for c in range(NA):
+        negate(c, sem["ld%d" % c], 16)
+    v.wait_ge(sem.ldb, 32)
+    for c in range(NP):
+        for h in pieces:
+            v.tensor_copy(T.xf[:, cols[c][h]], T.xs[:, cols[c][h]]).then_inc(sem["cp%d" % c], 1)
+    own(0)
+    own(1)
+    last(0)
+    for c in range(NA, NP):
+        own(c)
+    last(1)
+    for c in range(NA, NP):
+        last(c)
+
+    for c, qu in ((0, g.sync), (1, g.sync), (2, g.scalar), (3, g.sync), (4, g.scalar)):
         qu.wait_ge(sem["fin%d" % c], 2)
         qu.dma_start(T.y[:, pcols[c]], T.out[:, pcols[c]]).then_inc(sem.st, 16)
 

from concourse.bass import DstId, RemoteDMATransfer
from concourse.mybir import AluOpType

C = 1024
WORLD = 512
PARTS = ((384, 640), (0, 192), (192, 384), (640, 832), (832, 1024))
NA = 2
NP = len(PARTS)
NH = NP - NA
WZ = max((b - a) // 2 for a, b in PARTS)

SCRATCH = {
    "xs": ("sbuf", [128, C], "bfloat16"),
    "nx": ("sbuf", [128, C], "bfloat16"),
    "r1": ("sbuf", [128, C], "bfloat16"),
    "r2": ("sbuf", [128, C], "bfloat16"),
    "out": ("sbuf", [128, C], "bfloat16"),
    "zero": ("psum", [128, WZ], "float32"),
    "xf": ("psum", [128, C], "float32"),
    "own": ("psum", [128, C], "float32"),
}
SEMAPHORES = ["z", "sent", "st", "hx", "h1", "ldb"] + [n + str(c) for c in range(NP)
                                                       for n in ("ld", "ng", "cp", "a1_", "a2_", "ow", "fin")]


def _neighbours(c, cores, topo):
    near = far = None
    for d in cores:
        if d == c or not topo.may_write(c, d):
            continue
        if topo.same_plane(c, d):
            near = d
        elif topo.rack(topo.host(c)) != topo.rack(topo.host(d)):
            far = d
    return near, far


def _helpers(c, topo):
    chip = [k for k in range(WORLD) if topo.host(k) == topo.host(c) and topo.chip(k) == topo.chip(c)]
    mate = [k for k in range(WORLD) if topo.mates(c, k)][0]

    def kind(k):
        return (topo.die(k) != topo.die(c), not topo.may_write(k, mate))

    first = {}
    for k in chip:
        if kind(k) != kind(c) and kind(k) not in first:
            first[kind(k)] = k
    return [first[kd] for kd in sorted(first)]


def _bits(m):
    return [b for b in range(16) if (m >> b) & 1]


def _pack(sel):
    return sum(1 << b for b in sel), len(sel)


def _lanes(src, dst, which, topo):
    return _pack(_bits(topo.mask(src, dst))[which::2])


def _hand_lanes(c, helpers, j, off, topo):
    h = helpers[j]
    outer = topo.mask(c, off)
    if topo.die(h) == topo.die(c):
        return _pack(_bits(topo.mask(c, h) & outer))
    others = [k for k in helpers if topo.die(k) != topo.die(c)]
    return _pack(_bits(topo.mask(c, h) & ~outer)[others.index(h)::len(others)])


def _back_lanes(h, c, off, topo):
    return _pack(_bits(topo.mask(h, c) & ~topo.mask(h, off)))


def rank_program(g, core, T, topo):
    helpers_of = {c: _helpers(c, topo) for c in T.cores}
    owner = {h: (c, j) for c, hs in helpers_of.items() for j, h in enumerate(hs)}
    if T.rank_of(core) is None and core not in owner:
        return
    me = core if T.rank_of(core) is not None else owner[core][0]
    r = T.rank_of(me)
    sign = T.tables["SIGN"]
    sem = T.sem
    v = g.vector
    pieces = (0, 1)
    pcols = [slice(a, b) for a, b in PARTS]
    cols = [[slice(a + h * (b - a) // 2, a + (h + 1) * (b - a) // 2) for h in pieces] for a, b in PARTS]
    wid = [(b - a) // 2 for a, b in PARTS]

    mine = _neighbours(me, T.cores, topo)
    p = [mine[h] for h in pieces]
    q = [mine[1 - h] for h in pieces]
    rp = [T.rank_of(c) for c in p]
    rq = [T.rank_of(c) for c in q]
    rel = [sign[rq[h]][rp[h]] * sign[rq[h]][r] for h in pieces]
    n_neg = sum(1 for h in pieces if rel[h] < 0)
    s_m = [sign[r][T.rank_of(_neighbours(q[h], T.cores, topo)[h])] for h in pieces]
    n_out = [0]

    def transfer(dst, lanes, remote_sem, srcs, out):
        rid, pid = topo.addr(dst, core)
        m, n = lanes
        n_out[0] += n
        if len(srcs) == 1:
            return RemoteDMATransfer(dst_ids=[DstId(rid=rid, pnc=pid)], dma_engine_mask=m, remote_sem=remote_sem,
                                     src=srcs[0], dst=out, alu_op=0)
        return RemoteDMATransfer(dst_ids=[DstId(rid=rid, pnc=pid)], dma_engine_mask=m, remote_sem=remote_sem,
                                 srcs=srcs, dsts=[out], alu_op=1)

    def negate(c, ready, count):
        v.wait_ge(ready, count)
        for h in pieces:
            if rel[h] < 0:
                v.tensor_tensor(T.nx[:, cols[c][h]], T.zero[:, 0:wid[c]], T.xs[:, cols[c][h]],
                                AluOpType.subtract).then_inc(sem["ng%d" % c], 1)

    def fold_srcs(c, h):
        return [T.r1[:, cols[c][h]], (T.xs if rel[h] > 0 else T.nx)[:, cols[c][h]]]

    if n_neg:
        v.memset(T.zero[:], 0.0).then_inc(sem.z, 1)
        v.wait_ge(sem.z, 1)

    if core != me:
        j = owner[core][1]
        c = NA + j
        peer = [helpers_of[p[h]][j] for h in pieces]
        n_hx = _hand_lanes(me, helpers_of[me], j, p[0], topo)[1]
        n_h1 = sum(_lanes(peer[h], core, h, topo)[1] for h in pieces)
        g.wait_ge(sem.hx, n_hx)
        g.remote_dma_fused([transfer(peer[h], _lanes(core, peer[h], h, topo), sem.h1,
                                     [T.xs[:, cols[c][h]]], T.r1[:, cols[c][h]]) for h in pieces], local_sem=sem.sent)
        negate(c, sem.hx, n_hx)
        g.wait_ge(sem.h1, n_h1)
        if n_neg:
            g.wait_ge(sem["ng%d" % c], n_neg)
        g.remote_dma_fused([transfer(q[h], _lanes(core, q[h], 1 - h, topo), sem["a2_%d" % c],
                                     fold_srcs(c, h), T.r2[:, cols[c][h]]) for h in pieces], local_sem=sem.sent)
        g.remote_dma_fused([transfer(me, _back_lanes(core, me, q[0], topo), sem["a1_%d" % c],
                                     [T.r1[:, pcols[c]]], T.r1[:, pcols[c]])], local_sem=sem.sent)
        g.wait_ge(sem.sent, n_out[0])
        return

    hs = helpers_of[core]
    n_in1 = [sum(_lanes(p[h], core, h, topo)[1] for h in pieces)] * NA
    n_in2 = [sum(_lanes(q[h], core, 1 - h, topo)[1] for h in pieces)] * NA
    for j in range(NH):
        n_in1.append(_back_lanes(hs[j], core, q[0], topo)[1])
        n_in2.append(sum(_lanes(helpers_of[q[h]][j], core, 1 - h, topo)[1] for h in pieces))

    b12 = slice(PARTS[NA + 1][0], PARTS[NA + 2][1])
    g.sync.dma_start(T.xs[:, b12], T.x[:, b12]).then_inc(sem.ldb, 16)
    g.scalar.dma_start(T.xs[:, pcols[NA]], T.x[:, pcols[NA]]).then_inc(sem.ldb, 16)
    g.scalar.dma_start(T.xs[:, pcols[0]], T.x[:, pcols[0]]).then_inc(sem.ld0, 16)
    g.sync.dma_start(T.xs[:, pcols[1]], T.x[:, pcols[1]]).then_inc(sem.ld1, 16)

    g.wait_ge(sem.ldb, 32)
    g.remote_dma_fused([transfer(hs[j], _hand_lanes(core, hs, j, p[0], topo), sem.hx,
                                 [T.xs[:, pcols[NA + j]]], T.xs[:, pcols[NA + j]]) for j in range(NH)],
                       local_sem=sem.sent)
    for c in range(NA):
        g.wait_ge(sem["ld%d" % c], 16)
        g.remote_dma_fused([transfer(p[h], _lanes(core, p[h], h, topo), sem["a1_%d" % c],
                                     [T.xs[:, cols[c][h]]], T.r1[:, cols[c][h]]) for h in pieces], local_sem=sem.sent)
    for c in range(NA):
        g.wait_ge(sem["a1_%d" % c], n_in1[c])
        if n_neg:
            g.wait_ge(sem["ng%d" % c], n_neg)
        g.remote_dma_fused([transfer(q[h], _lanes(core, q[h], 1 - h, topo), sem["a2_%d" % c],
                                     fold_srcs(c, h), T.r2[:, cols[c][h]]) for h in pieces], local_sem=sem.sent)

    s_o = [1, 1]

    def own(c):
        v.wait_ge(sem["cp%d" % c], 2)
        v.wait_ge(sem["a1_%d" % c], n_in1[c])
        for h in pieces:
            a, b = sign[r][r], sign[r][rp[h]]
            mine_f, got, res = T.xf[:, cols[c][h]], T.r1[:, cols[c][h]], T.own[:, cols[c][h]]
            if a > 0:
                i = v.tensor_tensor(res, mine_f, got, AluOpType.add if b > 0 else AluOpType.subtract)
            elif b > 0:
                i = v.tensor_tensor(res, got, mine_f, AluOpType.subtract)
            else:
                i = v.tensor_tensor(res, mine_f, got, AluOpType.add)
                s_o[h] = -1
            i.then_inc(sem["ow%d" % c], 1)

    def last(c):
        v.wait_ge(sem["ow%d" % c], 2)
        v.wait_ge(sem["a2_%d" % c], n_in2[c])
        for h in pieces:
            assert s_o[h] > 0 or s_m[h] > 0
            part, got, res = T.own[:, cols[c][h]], T.r2[:, cols[c][h]], T.out[:, cols[c][h]]
            if s_o[h] > 0:
                i = v.tensor_tensor(res, part, got, AluOpType.add if s_m[h] > 0 else AluOpType.subtract)
            else:
                i = v.tensor_tensor(res, got, part, AluOpType.subtract)
            i.then_inc(sem["fin%d" % c], 1)

    for c in range(NA):
        negate(c, sem["ld%d" % c], 16)
    v.wait_ge(sem.ldb, 32)
    for c in range(NP):
        for h in pieces:
            v.tensor_copy(T.xf[:, cols[c][h]], T.xs[:, cols[c][h]]).then_inc(sem["cp%d" % c], 1)
    own(0)
    own(1)
    last(0)
    for c in range(NA, NP):
        own(c)
    last(1)
    for c in range(NA, NP):
        last(c)

    for c, qu in ((0, g.sync), (1, g.sync), (2, g.scalar), (3, g.sync), (4, g.scalar)):
        qu.wait_ge(sem["fin%d" % c], 2)
        qu.dma_start(T.y[:, pcols[c]], T.out[:, pcols[c]]).then_inc(sem.st, 16)

    g.wait_ge(sem.sent, n_out[0])
    g.wait_ge(sem.st, 16 * NP)
